import numpy as np
import ml_dtypes


def mxq(x, axis, fmt="e4m3"):
    dtype, down = {"e4m3": (ml_dtypes.float8_e4m3fn, 7), "e5m2": (ml_dtypes.float8_e5m2, 14)}[fmt]
    v = np.moveaxis(np.asarray(x, np.float32).astype(ml_dtypes.bfloat16).astype(np.float64), axis, -1)
    blocks = v.reshape(v.shape[:-1] + (-1, 32))
    amax = np.abs(blocks).max(-1, keepdims=True)
    byte = np.maximum(np.where(amax > 0, np.frexp(amax)[1] - 1 + 127, 0) - down, 1)
    scale = np.exp2(byte - 127.0)
    codes = (blocks / scale).astype(np.float32).astype(dtype).astype(np.float64)
    return np.moveaxis((codes * scale).reshape(v.shape), -1, axis)


WIDE = False


def mx_kscale(k):
    if not WIDE:
        return np.ones(k)
    levels = np.array([10, -10, 5, -5, 0])
    if k % 512:
        return np.exp2(np.random.permutation(np.resize(levels, k // 32))).repeat(32)
    a = np.empty((k // 512, 16))
    for p in range(k // 512):
        a[p, :8] = np.random.permutation(np.resize(levels, 8))
        for g in range(8):
            far = levels[np.abs(levels - a[p, g]) >= 10]
            a[p, g + 8] = far[np.random.randint(len(far))]
    return np.exp2(a.ravel()).repeat(32)


BF16 = ml_dtypes.bfloat16


def bf(x):
    return np.asarray(x, np.float32).astype(BF16)


def f64(x):
    return np.asarray(x).astype(np.float64)

def planes(Y):
    n, m = Y.shape
    b = f64(bf(Y)).reshape(n // 32, 32, m)
    amax = np.abs(b).max(1)
    byte = np.clip(np.where(amax > 0, np.frexp(amax)[1] - 1 + 127 - 7, 1), 1, 254)
    codes = (b * np.exp2(127.0 - byte)[:, None, :]).reshape(n, m).astype(np.float32).astype(ml_dtypes.float8_e4m3fn).view(np.uint8)
    words = codes.reshape(n // 512, 128, 4, m).transpose(0, 1, 3, 2)
    return np.ascontiguousarray(words), np.ascontiguousarray(byte.astype(np.uint8).reshape(n // 512, 16, m))


B, N = 1024, 1024

SMOOTH = 0.02


def contact_velocity(lam, g, d, c, b):
    p = mxq(lam * d[None, :], 1, "e4m3") @ mxq(g, 0, "e4m3")
    return c[None, :] * p + b


def setup_inputs():
    s, t = mx_kscale(N), mx_kscale(N)
    lam = np.random.standard_normal((B, N)) * 0.3
    g = np.random.standard_normal((N, N)) / np.sqrt(N)
    d = 1.0 + 0.1 * np.random.standard_normal(N)
    c = 1.0 + 0.1 * np.random.standard_normal(N)
    b = np.random.standard_normal((B, N)) * 0.15
    return {"lam": bf(lam), "g": bf(g / s[:, None] / t[None, :]), "d": bf(d * s), "c": bf(c * t), "b": bf(b)}


def core(lam, g, d, c, b):
    lam, g, d, c, b = f64(lam), f64(g), f64(d), f64(c), f64(b)
    w = contact_velocity(lam, g, d, c, b)
    r = np.sqrt(lam * lam + w * w + SMOOTH)
    phi = lam + w - r
    hl = (1.0 - lam / r) * phi
    hw = (1.0 - w / r) * phi
    back = mxq(hw * c[None, :], 1, "e4m3") @ mxq(g.T, 0, "e4m3")
    return hl + d[None, :] * back


def reference(lam, g, d, c, b):
    R_out = core(lam, g, d, c, b)
    words, scales = planes(R_out)
    return R_out, words, scales

@@ -1,0 +1,409 @@
+from contextlib import ExitStack
+
+import concourse.mybir as mybir
+from concourse.masks import make_identity
+
+S = 1024
+N = 1024
+P = 128
+PACK = 4
+GROUP = P * PACK
+EPS = 0.02
+TINY = 1e-30
+
+FLOPS = 2 * 2 * S * N * N
+
+F32 = mybir.dt.float32
+BF16 = mybir.dt.bfloat16
+U32 = mybir.dt.uint32
+I32 = mybir.dt.int32
+U8 = mybir.dt.uint8
+FP8X4 = mybir.dt.float8_e4m3fn_x4
+ALU = mybir.AluOpType
+ACTF = mybir.ActivationFunctionType
+
+
+def tile_fischerburmeisterlcpmeritgradientequilib_x1_kernel(tc, lam, g, d, c, b, out_0, out_1, out_2):
+    nc = tc.nc
+    with ExitStack() as ctx:
+        const = ctx.enter_context(tc.tile_pool(name="const", bufs=1))
+        big = ctx.enter_context(tc.tile_pool(name="big", bufs=1))
+        keep = ctx.enter_context(tc.tile_pool(name="keep", bufs=1))
+        grp = ctx.enter_context(tc.tile_pool(name="grp", bufs=4))
+        cod = ctx.enter_context(tc.tile_pool(name="cod", bufs=12))
+        unit = ctx.enter_context(tc.tile_pool(name="unit", bufs=4))
+        psum = ctx.enter_context(tc.psum_pool(name="psum", bufs=4))
+
+        ident = const.tile([P, P], F32, name="ident")
+        make_identity(nc, ident[:])
+
+        ctx.enter_context(tc.manual_schedule())
+
+        def new_codes():
+            words = cod.tile([P, GROUP], U32, name="words", tag="words", align_bytes=64)
+            rows = cod.tile([P, GROUP], U8, name="rows", tag="rows", align_bytes=64)
+            return words, rows
+
+        def quantize(grouped):
+            words, rows = new_codes()
+            nc.vector.quantize_mx(out=words[:].bitcast(FP8X4), scales=rows[:], in_=grouped[:])
+            return words, rows
+
+        def load_rows(x, group, cols, tile, slots=slice(0, PACK)):
+            view = x[group * GROUP:(group + 1) * GROUP, :].rearrange("(p t) i -> p t i", t=PACK)
+            nc.sync.dma_start(out=tile[:, slots, cols], in_=view[:, slots, cols])
+
+        def big_tile(tag):
+            return big.tile([P, PACK, N], BF16, name="nat_" + tag, tag=tag)
+
+        all_cols = slice(0, N)
+        lam_nat = [None, None]
+        b_nat = [None, None]
+        g_nat = [None, None]
+        lam_nat[0] = big_tile("big_a")
+        g_nat[0] = big_tile("big_c")
+        g_nat[1] = big_tile("big_d")
+        b_nat[0] = big_tile("big_b")
+        c_raw = const.tile([P, 2, PACK], BF16, name="c_raw")
+        d_raw = const.tile([P, 2, PACK], BF16, name="d_raw")
+        load_rows(lam, 0, all_cols, lam_nat[0], slice(0, 2))
+        load_rows(g, 0, slice(0, GROUP), g_nat[0])
+        load_rows(lam, 0, all_cols, lam_nat[0], slice(2, 4))
+        load_rows(g, 1, slice(0, GROUP), g_nat[1])
+        nc.sync.dma_start(out=d_raw[:], in_=d.rearrange("(g p t) -> p g t", p=P, t=PACK))
+        nc.sync.dma_start(out=c_raw[:], in_=c.rearrange("(g p t) -> p g t", p=P, t=PACK))
+        load_rows(b, 0, all_cols, b_nat[0])
+        load_rows(g, 0, slice(GROUP, N), g_nat[0])
+        load_rows(g, 1, slice(GROUP, N), g_nat[1])
+        lam_nat[1] = big_tile("big_a")
+        load_rows(lam, 1, all_cols, lam_nat[1])
+        b_nat[1] = big_tile("big_b")
+        load_rows(b, 1, all_cols, b_nat[1])
+
+        def turn(nat, k_group, slots):
+            bank = psum.tile([P, 2, 2 * P], F32, name="turned", tag="turn")
+            words = nat[:].bitcast(F32)
+            for n, slot in enumerate(slots):
+                for u in range(2):
+                    nc.tensor.transpose(bank[:, u, n * P:(n + 1) * P], words[:, slot, 256 * k_group + u:256 * (k_group + 1):2], ident[:])
+            return bank
+
+        def untangle(bank, dst, half):
+            nc.scalar.copy(
+                out=dst[:].rearrange("p (s t) -> p s t", t=PACK).bitcast(F32)[:, half * 2 * P:(half + 1) * 2 * P, :],
+                in_=bank[:].rearrange("p u r -> p r u"),
+            )
+
+        lamT = {}
+        bT = {}
+        gT = {}
+
+        def turn_pair(store, key, nat, k_group, half, pool, tag):
+            if half == 0:
+                store[key] = pool.tile([P, GROUP * PACK], BF16, name=tag, tag=tag, align_bytes=64, bufs=2 if tag == "bT" else 4)
+            bank = turn(nat, k_group, (2 * half, 2 * half + 1))
+            untangle(bank, store[key], half)
+
+        def turn_lam(gs, gi, half):
+            turn_pair(lamT, (gs, gi), lam_nat[gs], gi, half, unit, "lamT")
+
+        def turn_b(gs, gj, half):
+            turn_pair(bT, (gs, gj), b_nat[gs], gj, half, grp, "bT")
+
+        def turn_g(gj, gi, half):
+            turn_pair(gT, (gj, gi), g_nat[gi], gj, half, grp, "grouped")
+
+        g1 = {}
+        g1_codes = {}
+        gT_codes = {}
+        ld = {}
+        ld_codes = {}
+        hw_codes = {}
+
+        def group_g(gi, gj):
+            t = grp.tile([P, GROUP * PACK], BF16, name="g1", tag="grouped", align_bytes=64)
+            nc.vector.tensor_copy(
+                out=t[:].rearrange("p (j m i) -> p j m i", j=PACK, i=PACK),
+                in_=g_nat[gi][:, :, gj * GROUP:(gj + 1) * GROUP].rearrange("p i (m j) -> p j m i", j=PACK),
+            )
+            g1[gi, gj] = t
+
+        def scale_lam(gs, gi):
+            t = grp.tile([P, GROUP * PACK], BF16, name="lamd", tag="grouped", align_bytes=64)
+            nc.vector.tensor_tensor(
+                out=t[:].rearrange("p (s t) -> p s t", t=PACK),
+                in0=lamT[gs, gi][:].rearrange("p (s t) -> p s t", t=PACK),
+                in1=d_raw[:, gi, :].unsqueeze(1).to_broadcast([P, GROUP, PACK]),
+                op=ALU.mult,
+            )
+            ld[gs, gi] = t
+
+        def mx(bank, left, lcols, right, first, last):
+            nc.tensor.matmul_mx(
+                out=bank[:],
+                lhsT=left[0][:, lcols].bitcast(FP8X4),
+                lhsT_scale=left[1][:, lcols],
+                rhs=right[0][:].bitcast(FP8X4),
+                rhs_scale=right[1][:],
+                start=first,
+                stop=last,
+            )
+
+        p_banks = {}
+
+        def stage1(gs, gj):
+            for t in range(PACK):
+                bank = psum.tile([P, GROUP], F32, name="acc", tag="acc")
+                for gi in range(2):
+                    mx(bank, g1_codes[gi, gj], slice(t * P, (t + 1) * P), ld_codes[gs, gi], gi == 0, gi == 1)
+                p_banks[gs, gj, t] = bank
+
+        def unit_tile(tag):
+            return unit.tile([P, PACK, GROUP], F32, name=tag, tag=tag)
+
+        ta = {}
+        tb = {}
+        tcc = {}
+        td = {}
+        vecs = {}
+
+        def step_w(gs, gj):
+            ta[gs, gj] = unit_tile("ta")
+            bt = bT[gs, gj][:].rearrange("p (s t) -> p s t", t=PACK)
+            for t in range(PACK):
+                nc.vector.scalar_tensor_tensor(
+                    out=ta[gs, gj][:, t, :], in0=p_banks[gs, gj, t][:], scalar=vecs["c"][:, 4 * gj + t:4 * gj + t + 1],
+                    in1=bt[:, :, t], op0=ALU.mult, op1=ALU.add)
+
+        def lam_ts(gs, gj):
+            return lamT[gs, gj][:].rearrange("p (s t) -> p t s", t=PACK)
+
+        def step_l2(gs, gj):
+            tb[gs, gj] = unit_tile("tb")
+            nc.scalar.activation(out=tb[gs, gj][:], in_=lam_ts(gs, gj), func=ACTF.Square)
+
+        def step_w2(gs, gj):
+            tcc[gs, gj] = unit_tile("tcc")
+            nc.scalar.activation(out=tcc[gs, gj][:], in_=ta[gs, gj][:], func=ACTF.Square)
+
+        def step_s2(gs, gj):
+            nc.vector.scalar_tensor_tensor(
+                out=tb[gs, gj][:], in0=tcc[gs, gj][:], scalar=EPS, in1=tb[gs, gj][:], op0=ALU.add, op1=ALU.add)
+
+        def step_r(gs, gj):
+            nc.scalar.activation(out=tcc[gs, gj][:], in_=tb[gs, gj][:], func=ACTF.Sqrt)
+
+        def step_x(gs, gj):
+            td[gs, gj] = unit_tile("td")
+            nc.vector.tensor_tensor(out=td[gs, gj][:], in0=tcc[gs, gj][:], in1=lam_ts(gs, gj), op=ALU.subtract)
+
+        def step_y(gs, gj):
+            nc.vector.tensor_tensor(out=tcc[gs, gj][:], in0=tcc[gs, gj][:], in1=ta[gs, gj][:], op=ALU.subtract)
+
+        def step_phi(gs, gj):
+            nc.vector.tensor_tensor(out=ta[gs, gj][:], in0=ta[gs, gj][:], in1=td[gs, gj][:], op=ALU.subtract)
+
+        def step_ri(gs, gj):
+            nc.scalar.activation(out=tb[gs, gj][:], in_=tb[gs, gj][:], func=ACTF.Abs_reciprocal_sqrt)
+
+        def step_qc(gs, gj):
+            for t in range(PACK):
+                nc.vector.scalar_tensor_tensor(
+                    out=ta[gs, gj][:, t, :], in0=ta[gs, gj][:, t, :], scalar=vecs["c"][:, 4 * gj + t:4 * gj + t + 1],
+                    in1=tb[gs, gj][:, t, :], op0=ALU.mult, op1=ALU.mult)
+
+        hw = {}
+
+        def step_hw(gs, gj):
+            t = grp.tile([P, GROUP * PACK], BF16, name="hw", tag="grouped", align_bytes=64)
+            nc.vector.tensor_tensor(
+                out=t[:].rearrange("p (c i t) -> p c t i", i=4, t=PACK),
+                in0=ta[gs, gj][:].rearrange("p t (c i) -> p c t i", i=4),
+                in1=tcc[gs, gj][:].rearrange("p t (c i) -> p c t i", i=4),
+                op=ALU.mult)
+            hw[gs, gj] = t
+
+        def step_hl(gs, gj):
+            for t in range(PACK):
+                nc.vector.scalar_tensor_tensor(
+                    out=td[gs, gj][:, t, :], in0=ta[gs, gj][:, t, :], scalar=vecs["ic"][:, 4 * gj + t:4 * gj + t + 1],
+                    in1=td[gs, gj][:, t, :], op0=ALU.mult, op1=ALU.mult)
+
+        back = {}
+
+        def stage2(gs, gi):
+            for t in range(PACK):
+                bank = psum.tile([P, GROUP], F32, name="acc", tag="acc")
+                for gj in range(2):
+                    mx(bank, gT_codes[gj, gi], slice(t * P, (t + 1) * P), hw_codes[gs, gj], gj == 0, gj == 1)
+                back[gs, gi, t] = bank
+
+        outT = {}
+        out_nat = {}
+        out_rows = {}
+
+        def step_o(gs, gi):
+            outT[gs, gi] = big.tile([P, PACK, GROUP], F32, name="outT", tag=("big_c", "big_d")[gi])
+            for t in range(PACK):
+                nc.scalar.activation(
+                    out=outT[gs, gi][:, t, :], in_=back[gs, gi, t][:], func=ACTF.Copy, scale=vecs["d"][:, 4 * gi + t:4 * gi + t + 1])
+
+        def turn_out(gs, gi):
+            out_nat[gs, gi] = big.tile([P, PACK, GROUP], F32, name="out_nat", tag=("big_a", "big_b")[gi])
+            for ts in range(PACK):
+                bank = psum.tile([P, PACK, P], F32, name="turned", tag="turn")
+                for t in range(PACK):
+                    nc.tensor.matmul(bank[:, t, :], lhsT=outT[gs, gi][:, t, ts * P:(ts + 1) * P], rhs=ident[:], is_transpose=True, start=True, stop=False)
+                    nc.tensor.matmul(bank[:, t, :], lhsT=td[gs, gi][:, t, ts * P:(ts + 1) * P], rhs=ident[:], is_transpose=True, start=False, stop=True)
+                nc.scalar.copy(out=out_nat[gs, gi][:, ts, :].rearrange("p (m t) -> p m t", t=PACK), in_=bank[:].rearrange("p t m -> p m t"))
+            nc.sync.dma_start(
+                out=out_0[gs * GROUP:(gs + 1) * GROUP, gi * GROUP:(gi + 1) * GROUP].rearrange("(p t) i -> p t i", t=PACK),
+                in_=out_nat[gs, gi][:])
+
+        ob = {}
+
+        def step_ob(gs, gi, vector):
+            t = grp.tile([P, GROUP * PACK], BF16, name="ob", tag="grouped", align_bytes=64)
+            dst = t[:].rearrange("p (c i t) -> p c t i", i=4, t=PACK)
+            src = out_nat[gs, gi][:].rearrange("p t (c i) -> p c t i", i=4)
+            if vector:
+                nc.vector.tensor_copy(out=dst, in_=src)
+            else:
+                nc.scalar.copy(out=dst, in_=src)
+            ob[gs, gi] = t
+
+        def step_oq(gs, gi):
+            words, rows = new_codes()
+            nc.vector.quantize_mx(out=words[:].bitcast(FP8X4), scales=rows[:], in_=ob[gs, gi][:])
+            cols = slice(gi * GROUP, (gi + 1) * GROUP)
+            nc.sync.dma_start(out=out_1[gs, :, cols, :].rearrange("p m t -> p (m t)").bitcast(I32), in_=words[:].bitcast(I32))
+            for q in range(4):
+                nc.sync.dma_start(out=out_2[gs, 4 * q:4 * q + 4, cols].bitcast(I32), in_=rows[32 * q:32 * q + 4, :].bitcast(I32))
+
+        def prepare_vectors():
+            for name in ("c", "d", "pos", "neg", "m", "ic"):
+                vecs[name] = const.tile([P, 2 * PACK], F32, name="vec_" + name)
+            nc.vector.tensor_copy(out=vecs["d"][:], in_=d_raw[:].rearrange("p g t -> p (g t)"))
+            nc.vector.tensor_copy(out=vecs["m"][:], in_=c_raw[:].rearrange("p g t -> p (g t)"))
+            nc.vector.tensor_scalar_max(out=vecs["pos"][:], in0=vecs["m"][:], scalar1=TINY)
+            nc.vector.tensor_scalar_min(out=vecs["neg"][:], in0=vecs["m"][:], scalar1=-TINY)
+            nc.vector.tensor_single_scalar(out=vecs["m"][:], in_=vecs["m"][:], scalar=0.0, op=ALU.is_ge)
+            nc.vector.tensor_tensor(out=vecs["pos"][:], in0=vecs["pos"][:], in1=vecs["neg"][:], op=ALU.subtract)
+            nc.vector.tensor_tensor(out=vecs["pos"][:], in0=vecs["pos"][:], in1=vecs["m"][:], op=ALU.mult)
+            nc.vector.tensor_tensor(out=vecs["c"][:], in0=vecs["pos"][:], in1=vecs["neg"][:], op=ALU.add)
+            nc.vector.reciprocal(out=vecs["ic"][:], in_=vecs["c"][:])
+
+        for half in range(2):
+            for gi in range(2):
+                turn_lam(0, gi, half)
+        group_g(0, 0)
+        group_g(1, 0)
+        g1_codes[0, 0] = quantize(g1[0, 0])
+        scale_lam(0, 0)
+        g1_codes[1, 0] = quantize(g1[1, 0])
+        scale_lam(0, 1)
+        prepare_vectors()
+        ld_codes[0, 0] = quantize(ld[0, 0])
+        ld_codes[0, 1] = quantize(ld[0, 1])
+        stage1(0, 0)
+        turn_b(0, 0, 0)
+        turn_b(0, 0, 1)
+        step_l2(0, 0)
+        turn_b(0, 1, 0)
+        turn_b(0, 1, 1)
+        group_g(0, 1)
+        step_w(0, 0)
+        step_w2(0, 0)
+        group_g(1, 1)
+        g1_codes[0, 1] = quantize(g1[0, 1])
+        g1_codes[1, 1] = quantize(g1[1, 1])
+        stage1(0, 1)
+        step_l2(0, 1)
+        for half in range(2):
+            for gi in range(2):
+                turn_lam(1, gi, half)
+        step_s2(0, 0)
+        step_w(0, 1)
+        step_w2(0, 1)
+        step_r(0, 0)
+        scale_lam(1, 0)
+        scale_lam(1, 1)
+        ld_codes[1, 0] = quantize(ld[1, 0])
+        ld_codes[1, 1] = quantize(ld[1, 1])
+        step_s2(0, 1)
+        step_r(0, 1)
+        stage1(1, 0)
+        for half in range(2):
+            turn_b(1, 0, half)
+        step_l2(1, 0)
+        step_w(1, 0)
+        step_w2(1, 0)
+        stage1(1, 1)
+        for half in range(2):
+            turn_b(1, 1, half)
+        step_l2(1, 1)
+        step_w(1, 1)
+        step_w2(1, 1)
+        step_x(0, 0)
+        step_s2(1, 0)
+        step_r(1, 0)
+        step_x(0, 1)
+        step_s2(1, 1)
+        step_r(1, 1)
+        step_ri(0, 0)
+        step_ri(0, 1)
+        step_y(0, 0)
+        step_phi(0, 0)
+        step_y(0, 1)
+        step_phi(0, 1)
+        step_x(1, 0)
+        step_x(1, 1)
+        for gj in range(2):
+            for gi in range(2):
+                for half in range(2):
+                    turn_g(gj, gi, half)
+        step_qc(0, 0)
+        step_qc(0, 1)
+        for gj in range(2):
+            for gi in range(2):
+                gT_codes[gj, gi] = quantize(gT[gj, gi])
+        step_hw(0, 0)
+        step_hw(0, 1)
+        step_hl(0, 0)
+        hw_codes[0, 0] = quantize(hw[0, 0])
+        hw_codes[0, 1] = quantize(hw[0, 1])
+        stage2(0, 0)
+        step_hl(0, 1)
+        step_ri(1, 0)
+        step_ri(1, 1)
+        step_y(1, 0)
+        step_phi(1, 0)
+        step_o(0, 0)
+        turn_out(0, 0)
+        step_ob(0, 0, False)
+        stage2(0, 1)
+        step_y(1, 1)
+        step_phi(1, 1)
+        step_o(0, 1)
+        turn_out(0, 1)
+        step_ob(0, 1, False)
+        step_qc(1, 0)
+        step_qc(1, 1)
+        step_oq(0, 0)
+        step_hw(1, 0)
+        step_hw(1, 1)
+        hw_codes[1, 0] = quantize(hw[1, 0])
+        step_oq(0, 1)
+        hw_codes[1, 1] = quantize(hw[1, 1])
+        stage2(1, 0)
+        step_hl(1, 0)
+        step_hl(1, 1)
+        step_o(1, 0)
+        turn_out(1, 0)
+        stage2(1, 1)
+        step_o(1, 1)
+        turn_out(1, 1)
+        step_ob(1, 0, True)
+        step_oq(1, 0)
+        step_ob(1, 1, True)
+        step_oq(1, 1)

@@ -8,7 +8,7 @@ N = 1024
 P = 128
 PACK = 4
 GROUP = P * PACK
-EPS = 0.02
+SMOOTH = 0.02
 TINY = 1e-30
 
 FLOPS = 2 * 2 * S * N * N
@@ -20,390 +20,609 @@ I32 = mybir.dt.int32
 U8 = mybir.dt.uint8
 FP8X4 = mybir.dt.float8_e4m3fn_x4
 ALU = mybir.AluOpType
-ACTF = mybir.ActivationFunctionType
+FUNC = mybir.ActivationFunctionType
 
 
 def tile_fischerburmeisterlcpmeritgradientequilib_x1_kernel(tc, lam, g, d, c, b, out_0, out_1, out_2):
     nc = tc.nc
     with ExitStack() as ctx:
         const = ctx.enter_context(tc.tile_pool(name="const", bufs=1))
-        big = ctx.enter_context(tc.tile_pool(name="big", bufs=1))
-        keep = ctx.enter_context(tc.tile_pool(name="keep", bufs=1))
-        grp = ctx.enter_context(tc.tile_pool(name="grp", bufs=4))
-        cod = ctx.enter_context(tc.tile_pool(name="cod", bufs=12))
-        unit = ctx.enter_context(tc.tile_pool(name="unit", bufs=4))
+        natural = ctx.enter_context(tc.tile_pool(name="natural", bufs=1))
+        packed = ctx.enter_context(tc.tile_pool(name="packed", bufs=4))
+        quantized = ctx.enter_context(tc.tile_pool(name="quantized", bufs=4))
+        turned = ctx.enter_context(tc.tile_pool(name="turned", bufs=4))
         psum = ctx.enter_context(tc.psum_pool(name="psum", bufs=4))
 
-        ident = const.tile([P, P], F32, name="ident")
-        make_identity(nc, ident[:])
+        identity = const.tile([P, P], F32, name="identity")
+        make_identity(nc, identity[:])
 
         ctx.enter_context(tc.manual_schedule())
 
-        def new_codes():
-            words = cod.tile([P, GROUP], U32, name="words", tag="words", align_bytes=64)
-            rows = cod.tile([P, GROUP], U8, name="rows", tag="rows", align_bytes=64)
-            return words, rows
+        lam_rows, b_rows, g_rows = {}, {}, {}
 
-        def quantize(grouped):
-            words, rows = new_codes()
-            nc.vector.quantize_mx(out=words[:].bitcast(FP8X4), scales=rows[:], in_=grouped[:])
-            return words, rows
-
-        def load_rows(x, group, cols, tile, slots=slice(0, PACK)):
-            view = x[group * GROUP:(group + 1) * GROUP, :].rearrange("(p t) i -> p t i", t=PACK)
-            nc.sync.dma_start(out=tile[:, slots, cols], in_=view[:, slots, cols])
-
-        def big_tile(tag):
-            return big.tile([P, PACK, N], BF16, name="nat_" + tag, tag=tag)
-
-        all_cols = slice(0, N)
-        lam_nat = [None, None]
-        b_nat = [None, None]
-        g_nat = [None, None]
-        lam_nat[0] = big_tile("big_a")
-        g_nat[0] = big_tile("big_c")
-        g_nat[1] = big_tile("big_d")
-        b_nat[0] = big_tile("big_b")
-        c_raw = const.tile([P, 2, PACK], BF16, name="c_raw")
-        d_raw = const.tile([P, 2, PACK], BF16, name="d_raw")
-        load_rows(lam, 0, all_cols, lam_nat[0], slice(0, 2))
-        load_rows(g, 0, slice(0, GROUP), g_nat[0])
-        load_rows(lam, 0, all_cols, lam_nat[0], slice(2, 4))
-        load_rows(g, 1, slice(0, GROUP), g_nat[1])
-        nc.sync.dma_start(out=d_raw[:], in_=d.rearrange("(g p t) -> p g t", p=P, t=PACK))
-        nc.sync.dma_start(out=c_raw[:], in_=c.rearrange("(g p t) -> p g t", p=P, t=PACK))
-        load_rows(b, 0, all_cols, b_nat[0])
-        load_rows(g, 0, slice(GROUP, N), g_nat[0])
-        load_rows(g, 1, slice(GROUP, N), g_nat[1])
-        lam_nat[1] = big_tile("big_a")
-        load_rows(lam, 1, all_cols, lam_nat[1])
-        b_nat[1] = big_tile("big_b")
-        load_rows(b, 1, all_cols, b_nat[1])
-
-        def turn(nat, k_group, slots):
-            bank = psum.tile([P, 2, 2 * P], F32, name="turned", tag="turn")
-            words = nat[:].bitcast(F32)
-            for n, slot in enumerate(slots):
-                for u in range(2):
-                    nc.tensor.transpose(bank[:, u, n * P:(n + 1) * P], words[:, slot, 256 * k_group + u:256 * (k_group + 1):2], ident[:])
-            return bank
-
-        def untangle(bank, dst, half):
-            nc.scalar.copy(
-                out=dst[:].rearrange("p (s t) -> p s t", t=PACK).bitcast(F32)[:, half * 2 * P:(half + 1) * 2 * P, :],
-                in_=bank[:].rearrange("p u r -> p r u"),
+        def load_g(gi, gj):
+            g_rows[gi, gj] = natural.tile([P, PACK, GROUP], BF16, name="g_rows", tag="quarter", bufs=4)
+            nc.sync.dma_start(
+                out=g_rows[gi, gj][:],
+                in_=g[gi * GROUP : (gi + 1) * GROUP, gj * GROUP : (gj + 1) * GROUP].rearrange("(p t) j -> p t j", t=PACK),
             )
 
-        lamT = {}
-        bT = {}
-        gT = {}
+        def load_rows(x, gs, k, tile, slots=slice(0, PACK)):
+            rows = x[gs * GROUP : (gs + 1) * GROUP, k * GROUP : (k + 1) * GROUP].rearrange("(p t) i -> p t i", t=PACK)
+            nc.sync.dma_start(out=tile[:, k, slots, :], in_=rows[:, slots, :])
 
-        def turn_pair(store, key, nat, k_group, half, pool, tag):
-            if half == 0:
-                store[key] = pool.tile([P, GROUP * PACK], BF16, name=tag, tag=tag, align_bytes=64, bufs=2 if tag == "bT" else 4)
-            bank = turn(nat, k_group, (2 * half, 2 * half + 1))
-            untangle(bank, store[key], half)
+        def new_lam_rows(gs):
+            lam_rows[gs] = natural.tile([P, 2, PACK, GROUP], BF16, name="lam_rows", tag="lam_then_out")
+
+        def new_b_rows(gs):
+            b_rows[gs] = natural.tile([P, 2, PACK, GROUP], BF16, name="b_rows", tag="b_then_out")
+
+        def load_second_lam():
+            new_lam_rows(1)
+            for k in range(2):
+                load_rows(lam, 1, k, lam_rows[1])
+
+        def load_second_b():
+            new_b_rows(1)
+            for k in range(2):
+                load_rows(b, 1, k, b_rows[1])
+
+        new_lam_rows(0)
+        new_b_rows(0)
+        c_bf16 = const.tile([P, 2, PACK], BF16, name="c_bf16")
+        d_bf16 = const.tile([P, 2, PACK], BF16, name="d_bf16")
+        for k in range(2):
+            load_rows(lam, 0, k, lam_rows[0], slice(0, 2))
+        load_g(0, 0)
+        for k in range(2):
+            load_rows(lam, 0, k, lam_rows[0], slice(2, 4))
+        nc.sync.dma_start(out=d_bf16[:], in_=d.rearrange("(g p t) -> p g t", p=P, t=PACK))
+        load_g(1, 0)
+        nc.sync.dma_start(out=c_bf16[:], in_=c.rearrange("(g p t) -> p g t", p=P, t=PACK))
+        for k in range(2):
+            load_rows(b, 0, k, b_rows[0])
+        load_g(0, 1)
+        load_g(1, 1)
+
+        vectors = {}
+
+        def column(name, group, t):
+            return vectors[name][:, PACK * group + t : PACK * group + t + 1]
+
+        def prepare_vectors():
+            for name in ("c", "minus_d", "minus_c", "upper", "lower", "minus_1_over_c"):
+                vectors[name] = const.tile([P, 2 * PACK], F32, name="vector_" + name)
+            c_flat = c_bf16[:].rearrange("p g t -> p (g t)")
+            d_flat = d_bf16[:].rearrange("p g t -> p (g t)")
+            nc.gpsimd.tensor_scalar(out=vectors["minus_d"][:], in0=d_flat, scalar1=-1.0, scalar2=0.0, op0=ALU.mult, op1=ALU.add)
+            nc.gpsimd.tensor_scalar(out=vectors["c"][:], in0=c_flat, scalar1=0.0, scalar2=1.0, op0=ALU.is_ge, op1=ALU.mult)
+            nc.gpsimd.tensor_scalar(out=vectors["upper"][:], in0=c_flat, scalar1=TINY, scalar2=1.0, op0=ALU.max, op1=ALU.mult)
+            nc.gpsimd.tensor_scalar(out=vectors["lower"][:], in0=c_flat, scalar1=-TINY, scalar2=1.0, op0=ALU.min, op1=ALU.mult)
+            nc.gpsimd.tensor_tensor(out=vectors["upper"][:], in0=vectors["upper"][:], in1=vectors["lower"][:], op=ALU.subtract)
+            nc.gpsimd.tensor_tensor(out=vectors["upper"][:], in0=vectors["upper"][:], in1=vectors["c"][:], op=ALU.mult)
+            nc.gpsimd.tensor_tensor(out=vectors["c"][:], in0=vectors["upper"][:], in1=vectors["lower"][:], op=ALU.add)
+            nc.gpsimd.tensor_scalar(out=vectors["minus_c"][:], in0=vectors["c"][:], scalar1=-1.0, scalar2=0.0, op0=ALU.mult, op1=ALU.add)
+
+        def invert_c():
+            nc.vector.reciprocal(out=vectors["minus_1_over_c"][:], in_=vectors["minus_c"][:])
+
+        banks = {}
+        lam_t, b_t, g_t = {}, {}, {}
+
+        def turn(key, rows):
+            half = key[-1]
+            banks[key] = psum.tile([P, 2, 2 * P], F32, name="turn_bank", tag="turn")
+            words = rows.bitcast(F32)
+            for n in range(2):
+                for u in range(2):
+                    nc.tensor.transpose(banks[key][:, u, n * P : (n + 1) * P], words[:, 2 * half + n, u::2], identity[:])
 
         def turn_lam(gs, gi, half):
-            turn_pair(lamT, (gs, gi), lam_nat[gs], gi, half, unit, "lamT")
+            turn(("lam", gs, gi, half), lam_rows[gs][:, gi])
 
         def turn_b(gs, gj, half):
-            turn_pair(bT, (gs, gj), b_nat[gs], gj, half, grp, "bT")
+            turn(("b", gs, gj, half), b_rows[gs][:, gj])
 
         def turn_g(gj, gi, half):
-            turn_pair(gT, (gj, gi), g_nat[gi], gj, half, grp, "grouped")
+            turn(("g", gj, gi, half), g_rows[gi, gj][:])
 
-        g1 = {}
-        g1_codes = {}
-        gT_codes = {}
-        ld = {}
-        ld_codes = {}
-        hw_codes = {}
+        def copy_words(out, in_, on_vector):
+            (nc.vector.tensor_copy if on_vector else nc.scalar.copy)(out=out, in_=in_)
 
-        def group_g(gi, gj):
-            t = grp.tile([P, GROUP * PACK], BF16, name="g1", tag="grouped", align_bytes=64)
-            nc.vector.tensor_copy(
-                out=t[:].rearrange("p (j m i) -> p j m i", j=PACK, i=PACK),
-                in_=g_nat[gi][:, :, gj * GROUP:(gj + 1) * GROUP].rearrange("p i (m j) -> p j m i", j=PACK),
+        def take_words(store, key, bufs, pool, on_vector):
+            name, x, y, half = key
+            if (x, y) not in store:
+                store[x, y] = pool.tile([P, GROUP * PACK], BF16, name=name + "_t", tag=name + "_t", align_bytes=64, bufs=bufs)
+            words = store[x, y][:].rearrange("p (u s e) -> p u (s e)", u=2, e=2).bitcast(F32)
+            copy_words(words[:, :, half * 2 * P : (half + 1) * 2 * P], banks[key][:], on_vector)
+
+        def take_lam(gs, gi, half, on_vector=False):
+            take_words(lam_t, ("lam", gs, gi, half), 4, turned, on_vector)
+
+        def take_b(gs, gj, half, on_vector=False):
+            take_words(b_t, ("b", gs, gj, half), 2, packed, on_vector)
+
+        def new_packed(name):
+            return packed.tile([P, GROUP * PACK], BF16, name=name, tag="packed", align_bytes=64)
+
+        def take_g(gj, gi, half, on_vector=False):
+            if (gj, gi) not in g_t:
+                g_t[gj, gi] = new_packed("g_t")
+            words = g_t[gj, gi][:].rearrange("p (i t) -> p i t", t=PACK).bitcast(F32)
+            copy_words(words[:, half * 2 * P : (half + 1) * 2 * P, :], banks["g", gj, gi, half][:].rearrange("p u r -> p r u"), on_vector)
+
+        def by_t(tile):
+            return tile[:].rearrange("p (u s e) -> p u e s", u=2, e=2)
+
+        def split_t(tile):
+            return tile[:].rearrange("p (u e) s -> p u e s", e=2)
+
+        g_codes, g_t_codes, lam_d_codes, hw_codes = {}, {}, {}, {}
+        g_packed, lam_d = {}, {}
+
+        def quantize(values, kind):
+            words = quantized.tile([P, GROUP], U32, name="words", tag="words_" + kind, align_bytes=64)
+            scales = quantized.tile([P, GROUP], U8, name="scales", tag="scales_" + kind, align_bytes=64)
+            nc.vector.quantize_mx(out=words[:].bitcast(FP8X4), scales=scales[:], in_=values[:])
+            return words, scales
+
+        def group_g(gi, gj, on_scalar=False):
+            g_packed[gi, gj] = new_packed("g_packed")
+            (nc.scalar.copy if on_scalar else nc.vector.tensor_copy)(
+                out=g_packed[gi, gj][:].rearrange("p (t m i) -> p t m i", t=PACK, i=PACK),
+                in_=g_rows[gi, gj][:].rearrange("p i (m t) -> p t m i", t=PACK),
             )
-            g1[gi, gj] = t
+
+        def quantize_g(gi, gj):
+            g_codes[gi, gj] = quantize(g_packed[gi, gj], "g")
+
+        def quantize_g_t(gj, gi):
+            g_t_codes[gj, gi] = quantize(g_t[gj, gi], "g")
 
         def scale_lam(gs, gi):
-            t = grp.tile([P, GROUP * PACK], BF16, name="lamd", tag="grouped", align_bytes=64)
+            lam_d[gs, gi] = new_packed("lam_d")
             nc.vector.tensor_tensor(
-                out=t[:].rearrange("p (s t) -> p s t", t=PACK),
-                in0=lamT[gs, gi][:].rearrange("p (s t) -> p s t", t=PACK),
-                in1=d_raw[:, gi, :].unsqueeze(1).to_broadcast([P, GROUP, PACK]),
+                out=lam_d[gs, gi][:].rearrange("p (s u e) -> p s u e", u=2, e=2),
+                in0=lam_t[gs, gi][:].rearrange("p (u s e) -> p s u e", u=2, e=2),
+                in1=d_bf16[:, gi, :].rearrange("p (u e) -> p u e", e=2).unsqueeze(1).to_broadcast([P, GROUP, 2, 2]),
                 op=ALU.mult,
             )
-            ld[gs, gi] = t
 
-        def mx(bank, left, lcols, right, first, last):
+        def quantize_lam_d(gs, gi):
+            lam_d_codes[gs, gi] = quantize(lam_d[gs, gi], "samples")
+
+        products = {}
+
+        def pass_mx(bank, left, t, right, first, last):
+            cols = slice(t * P, (t + 1) * P)
             nc.tensor.matmul_mx(
                 out=bank[:],
-                lhsT=left[0][:, lcols].bitcast(FP8X4),
-                lhsT_scale=left[1][:, lcols],
+                lhsT=left[0][:, cols].bitcast(FP8X4),
+                lhsT_scale=left[1][:, cols],
                 rhs=right[0][:].bitcast(FP8X4),
                 rhs_scale=right[1][:],
                 start=first,
                 stop=last,
             )
 
-        p_banks = {}
+        def first_product(gs, gj, t):
+            products[gs, gj, t] = psum.tile([P, GROUP], F32, name="product", tag="product")
+            for gi in range(2):
+                pass_mx(products[gs, gj, t], g_codes[gi, gj], t, lam_d_codes[gs, gi], gi == 0, gi == 1)
 
-        def stage1(gs, gj):
-            for t in range(PACK):
-                bank = psum.tile([P, GROUP], F32, name="acc", tag="acc")
-                for gi in range(2):
-                    mx(bank, g1_codes[gi, gj], slice(t * P, (t + 1) * P), ld_codes[gs, gi], gi == 0, gi == 1)
-                p_banks[gs, gj, t] = bank
+        w_tile, sum_tile, root_tile, term_tile, w_squared, qc_tile = {}, {}, {}, {}, {}, {}
 
-        def unit_tile(tag):
-            return unit.tile([P, PACK, GROUP], F32, name=tag, tag=tag)
+        def new_turned(name, tag, bufs=4):
+            return turned.tile([P, PACK, GROUP], F32, name=name, tag=tag, bufs=bufs)
 
-        ta = {}
-        tb = {}
-        tcc = {}
-        td = {}
-        vecs = {}
-
-        def step_w(gs, gj):
-            ta[gs, gj] = unit_tile("ta")
-            bt = bT[gs, gj][:].rearrange("p (s t) -> p s t", t=PACK)
-            for t in range(PACK):
-                nc.vector.scalar_tensor_tensor(
-                    out=ta[gs, gj][:, t, :], in0=p_banks[gs, gj, t][:], scalar=vecs["c"][:, 4 * gj + t:4 * gj + t + 1],
-                    in1=bt[:, :, t], op0=ALU.mult, op1=ALU.add)
-
-        def lam_ts(gs, gj):
-            return lamT[gs, gj][:].rearrange("p (s t) -> p t s", t=PACK)
-
-        def step_l2(gs, gj):
-            tb[gs, gj] = unit_tile("tb")
-            nc.scalar.activation(out=tb[gs, gj][:], in_=lam_ts(gs, gj), func=ACTF.Square)
-
-        def step_w2(gs, gj):
-            tcc[gs, gj] = unit_tile("tcc")
-            nc.scalar.activation(out=tcc[gs, gj][:], in_=ta[gs, gj][:], func=ACTF.Square)
-
-        def step_s2(gs, gj):
+        def minus_w(gs, gj, t):
+            if (gs, gj) not in w_tile:
+                w_tile[gs, gj] = new_turned("w_tile", "w")
             nc.vector.scalar_tensor_tensor(
-                out=tb[gs, gj][:], in0=tcc[gs, gj][:], scalar=EPS, in1=tb[gs, gj][:], op0=ALU.add, op1=ALU.add)
+                out=w_tile[gs, gj][:, t, :],
+                in0=products[gs, gj, t][:],
+                scalar=column("minus_c", gj, t),
+                in1=by_t(b_t[gs, gj])[:, t // 2, t % 2, :],
+                op0=ALU.mult,
+                op1=ALU.subtract,
+            )
 
-        def step_r(gs, gj):
-            nc.scalar.activation(out=tcc[gs, gj][:], in_=tb[gs, gj][:], func=ACTF.Sqrt)
+        def square_lam(gs, gj):
+            sum_tile[gs, gj] = new_turned("sum_tile", "sum")
+            nc.scalar.activation(out=split_t(sum_tile[gs, gj]), in_=by_t(lam_t[gs, gj]), func=FUNC.Square)
 
-        def step_x(gs, gj):
-            td[gs, gj] = unit_tile("td")
-            nc.vector.tensor_tensor(out=td[gs, gj][:], in0=tcc[gs, gj][:], in1=lam_ts(gs, gj), op=ALU.subtract)
+        def square_w(gs, gj):
+            w_squared[gs, gj] = new_turned("w_squared", "short", 2)
+            nc.scalar.activation(out=w_squared[gs, gj][:], in_=w_tile[gs, gj][:], func=FUNC.Square)
 
-        def step_y(gs, gj):
-            nc.vector.tensor_tensor(out=tcc[gs, gj][:], in0=tcc[gs, gj][:], in1=ta[gs, gj][:], op=ALU.subtract)
+        def sum_squares(gs, gj):
+            nc.vector.scalar_tensor_tensor(
+                out=sum_tile[gs, gj][:], in0=w_squared[gs, gj][:], scalar=SMOOTH, in1=sum_tile[gs, gj][:], op0=ALU.add, op1=ALU.add
+            )
 
-        def step_phi(gs, gj):
-            nc.vector.tensor_tensor(out=ta[gs, gj][:], in0=ta[gs, gj][:], in1=td[gs, gj][:], op=ALU.subtract)
+        def root(gs, gj):
+            root_tile[gs, gj] = new_turned("root_tile", "root")
+            nc.scalar.activation(out=root_tile[gs, gj][:], in_=sum_tile[gs, gj][:], func=FUNC.Sqrt)
 
-        def step_ri(gs, gj):
-            nc.scalar.activation(out=tb[gs, gj][:], in_=tb[gs, gj][:], func=ACTF.Abs_reciprocal_sqrt)
+        def inverse_root(gs, gj):
+            nc.scalar.activation(out=sum_tile[gs, gj][:], in_=sum_tile[gs, gj][:], func=FUNC.Abs_reciprocal_sqrt)
 
-        def step_qc(gs, gj):
+        def minus_lam_w(gs, gj):
+            term_tile[gs, gj] = new_turned("term_tile", "term")
+            nc.vector.tensor_tensor(out=split_t(term_tile[gs, gj]), in0=split_t(w_tile[gs, gj]), in1=by_t(lam_t[gs, gj]), op=ALU.subtract)
+
+        def r_minus_w_0(gs, gj):
+            nc.vector.tensor_tensor(out=w_tile[gs, gj][:], in0=root_tile[gs, gj][:], in1=w_tile[gs, gj][:], op=ALU.add)
+
+        def ratio(gs, gj):
+            nc.vector.scalar_tensor_tensor(
+                out=sum_tile[gs, gj][:], in0=term_tile[gs, gj][:], scalar=-1.0, in1=sum_tile[gs, gj][:], op0=ALU.mult, op1=ALU.mult
+            )
+
+        def qc_0(gs, gj):
+            qc_tile[gs, gj] = new_turned("qc_tile", "short", 2)
+            for t in range(PACK):
+                nc.scalar.activation(
+                    out=qc_tile[gs, gj][:, t, :],
+                    in_=sum_tile[gs, gj][:, t, :],
+                    func=FUNC.Identity,
+                    scale=column("c", gj, t),
+                    bias=column("minus_c", gj, t),
+                )
+
+        def lam_q(gs, gj):
+            for u in range(2):
+                part = split_t(sum_tile[gs, gj])[:, u]
+                nc.vector.scalar_tensor_tensor(
+                    out=part, in0=part, scalar=1.0, in1=by_t(lam_t[gs, gj])[:, u], op0=ALU.subtract, op1=ALU.mult
+                )
+
+        def r_minus_lam(gs, gj):
+            term_tile[gs, gj] = new_turned("term_tile", "term")
+            nc.vector.tensor_tensor(out=split_t(term_tile[gs, gj]), in0=split_t(root_tile[gs, gj]), in1=by_t(lam_t[gs, gj]), op=ALU.subtract)
+
+        def r_minus_w_1(gs, gj):
+            nc.vector.tensor_tensor(out=root_tile[gs, gj][:], in0=root_tile[gs, gj][:], in1=w_tile[gs, gj][:], op=ALU.add)
+
+        def minus_phi(gs, gj):
+            nc.vector.tensor_tensor(out=w_tile[gs, gj][:], in0=w_tile[gs, gj][:], in1=term_tile[gs, gj][:], op=ALU.add)
+
+        def qc_1(gs, gj):
             for t in range(PACK):
                 nc.vector.scalar_tensor_tensor(
-                    out=ta[gs, gj][:, t, :], in0=ta[gs, gj][:, t, :], scalar=vecs["c"][:, 4 * gj + t:4 * gj + t + 1],
-                    in1=tb[gs, gj][:, t, :], op0=ALU.mult, op1=ALU.mult)
+                    out=w_tile[gs, gj][:, t, :],
+                    in0=w_tile[gs, gj][:, t, :],
+                    scalar=column("minus_c", gj, t),
+                    in1=sum_tile[gs, gj][:, t, :],
+                    op0=ALU.mult,
+                    op1=ALU.mult,
+                )
 
-        hw = {}
+        def minus_hl(gs, gj):
+            for t in range(PACK):
+                nc.vector.scalar_tensor_tensor(
+                    out=term_tile[gs, gj][:, t, :],
+                    in0=w_tile[gs, gj][:, t, :],
+                    scalar=column("minus_1_over_c", gj, t),
+                    in1=term_tile[gs, gj][:, t, :],
+                    op0=ALU.mult,
+                    op1=ALU.mult,
+                )
 
-        def step_hw(gs, gj):
-            t = grp.tile([P, GROUP * PACK], BF16, name="hw", tag="grouped", align_bytes=64)
+        hw_c = {}
+
+        def interleave(tile):
+            return tile[:].rearrange("p t (n k) -> p n t k", k=4)
+
+        def interleaved(tile):
+            return tile[:].rearrange("p (n k t) -> p n t k", k=4, t=PACK)
+
+        def multiply_hw_c(gs, gj):
+            hw_c[gs, gj] = new_packed("hw_c")
+            qc, r_minus_w = (qc_tile, w_tile) if gs == 0 else (w_tile, root_tile)
             nc.vector.tensor_tensor(
-                out=t[:].rearrange("p (c i t) -> p c t i", i=4, t=PACK),
-                in0=ta[gs, gj][:].rearrange("p t (c i) -> p c t i", i=4),
-                in1=tcc[gs, gj][:].rearrange("p t (c i) -> p c t i", i=4),
-                op=ALU.mult)
-            hw[gs, gj] = t
+                out=interleaved(hw_c[gs, gj]), in0=interleave(qc[gs, gj]), in1=interleave(r_minus_w[gs, gj]), op=ALU.mult
+            )
 
-        def step_hl(gs, gj):
-            for t in range(PACK):
-                nc.vector.scalar_tensor_tensor(
-                    out=td[gs, gj][:, t, :], in0=ta[gs, gj][:, t, :], scalar=vecs["ic"][:, 4 * gj + t:4 * gj + t + 1],
-                    in1=td[gs, gj][:, t, :], op0=ALU.mult, op1=ALU.mult)
+        def quantize_hw(gs, gj):
+            hw_codes[gs, gj] = quantize(hw_c[gs, gj], "samples")
 
         back = {}
 
-        def stage2(gs, gi):
-            for t in range(PACK):
-                bank = psum.tile([P, GROUP], F32, name="acc", tag="acc")
-                for gj in range(2):
-                    mx(bank, gT_codes[gj, gi], slice(t * P, (t + 1) * P), hw_codes[gs, gj], gj == 0, gj == 1)
-                back[gs, gi, t] = bank
+        def second_product(gs, gi, t, gj):
+            if gj == 0:
+                back[gs, gi, t] = psum.tile([P, GROUP], F32, name="product", tag="product")
+            pass_mx(back[gs, gi, t], g_t_codes[gj, gi], t, hw_codes[gs, gj], gj == 0, gj == 1)
 
-        outT = {}
-        out_nat = {}
-        out_rows = {}
+        minus_d_back = {}
 
-        def step_o(gs, gi):
-            outT[gs, gi] = big.tile([P, PACK, GROUP], F32, name="outT", tag=("big_c", "big_d")[gi])
-            for t in range(PACK):
-                nc.scalar.activation(
-                    out=outT[gs, gi][:, t, :], in_=back[gs, gi, t][:], func=ACTF.Copy, scale=vecs["d"][:, 4 * gi + t:4 * gi + t + 1])
-
-        def turn_out(gs, gi):
-            out_nat[gs, gi] = big.tile([P, PACK, GROUP], F32, name="out_nat", tag=("big_a", "big_b")[gi])
-            for ts in range(PACK):
-                bank = psum.tile([P, PACK, P], F32, name="turned", tag="turn")
-                for t in range(PACK):
-                    nc.tensor.matmul(bank[:, t, :], lhsT=outT[gs, gi][:, t, ts * P:(ts + 1) * P], rhs=ident[:], is_transpose=True, start=True, stop=False)
-                    nc.tensor.matmul(bank[:, t, :], lhsT=td[gs, gi][:, t, ts * P:(ts + 1) * P], rhs=ident[:], is_transpose=True, start=False, stop=True)
-                nc.scalar.copy(out=out_nat[gs, gi][:, ts, :].rearrange("p (m t) -> p m t", t=PACK), in_=bank[:].rearrange("p t m -> p m t"))
-            nc.sync.dma_start(
-                out=out_0[gs * GROUP:(gs + 1) * GROUP, gi * GROUP:(gi + 1) * GROUP].rearrange("(p t) i -> p t i", t=PACK),
-                in_=out_nat[gs, gi][:])
-
-        ob = {}
-
-        def step_ob(gs, gi, vector):
-            t = grp.tile([P, GROUP * PACK], BF16, name="ob", tag="grouped", align_bytes=64)
-            dst = t[:].rearrange("p (c i t) -> p c t i", i=4, t=PACK)
-            src = out_nat[gs, gi][:].rearrange("p t (c i) -> p c t i", i=4)
-            if vector:
-                nc.vector.tensor_copy(out=dst, in_=src)
+        def scale_back(gs, gi, t, on_vector=False):
+            if (gs, gi, t // 2) not in minus_d_back:
+                minus_d_back[gs, gi, t // 2] = natural.tile([P, 2, GROUP], F32, name="minus_d_back", tag="quarter", bufs=4)
+            target = minus_d_back[gs, gi, t // 2][:, t % 2, :]
+            if on_vector:
+                nc.vector.tensor_scalar_mul(out=target, in0=back[gs, gi, t][:], scalar1=column("minus_d", gi, t))
             else:
-                nc.scalar.copy(out=dst, in_=src)
-            ob[gs, gi] = t
+                nc.scalar.activation(out=target, in_=back[gs, gi, t][:], func=FUNC.Copy, scale=column("minus_d", gi, t))
 
-        def step_oq(gs, gi):
-            words, rows = new_codes()
-            nc.vector.quantize_mx(out=words[:].bitcast(FP8X4), scales=rows[:], in_=ob[gs, gi][:])
+        out_banks, out_rows, out_packed = {}, {}, {}
+
+        def add_turned(gs, gi, slot):
+            bank = psum.tile([P, PACK, P], F32, name="out_bank", tag="turn")
+            for t in range(PACK):
+                addends = [term_tile[gs, gi][:, t, :], minus_d_back[gs, gi, t // 2][:, t % 2, :]]
+                if gs == 0:
+                    addends += [root_tile[gs, gi][:, t, :], sum_tile[gs, gi][:, t, :]]
+                for n, addend in enumerate(addends):
+                    nc.tensor.matmul(
+                        bank[:, t, :],
+                        lhsT=addend[:, slot * P : (slot + 1) * P],
+                        rhs=identity[:],
+                        is_transpose=True,
+                        start=n == 0,
+                        stop=n == len(addends) - 1,
+                    )
+            out_banks[gs, gi, slot] = bank
+
+        def copy_out(gs, gi, slot, on_vector=False):
+            if (gs, gi) not in out_rows:
+                out_rows[gs, gi] = natural.tile([P, PACK, GROUP], F32, name="out_rows", tag=("lam_then_out", "b_then_out")[gi])
+            target = out_rows[gs, gi][:, slot, :].rearrange("p (m t) -> p m t", t=PACK)
+            source = out_banks[gs, gi, slot][:].rearrange("p t m -> p m t")
+            if on_vector:
+                nc.vector.tensor_scalar_mul(out=target, in0=source, scalar1=-1.0)
+            else:
+                nc.scalar.activation(out=target, in_=source, func=FUNC.Copy, scale=-1.0)
+
+        def store_out(gs, gi):
+            nc.sync.dma_start(
+                out=out_0[gs * GROUP : (gs + 1) * GROUP, gi * GROUP : (gi + 1) * GROUP].rearrange("(p t) i -> p t i", t=PACK),
+                in_=out_rows[gs, gi][:],
+            )
+
+        def pack_out(gs, gi, on_vector):
+            out_packed[gs, gi] = new_packed("out_packed")
+            copy = nc.vector.tensor_copy if on_vector else nc.scalar.copy
+            copy(out=interleaved(out_packed[gs, gi]), in_=interleave(out_rows[gs, gi]))
+
+        def quantize_out(gs, gi):
+            words, scales = quantize(out_packed[gs, gi], "samples")
             cols = slice(gi * GROUP, (gi + 1) * GROUP)
             nc.sync.dma_start(out=out_1[gs, :, cols, :].rearrange("p m t -> p (m t)").bitcast(I32), in_=words[:].bitcast(I32))
-            for q in range(4):
-                nc.sync.dma_start(out=out_2[gs, 4 * q:4 * q + 4, cols].bitcast(I32), in_=rows[32 * q:32 * q + 4, :].bitcast(I32))
+            for quadrant in range(4):
+                nc.sync.dma_start(
+                    out=out_2[gs, 4 * quadrant : 4 * quadrant + 4, cols].bitcast(I32),
+                    in_=scales[32 * quadrant : 32 * quadrant + 4, :].bitcast(I32),
+                )
 
-        def prepare_vectors():
-            for name in ("c", "d", "pos", "neg", "m", "ic"):
-                vecs[name] = const.tile([P, 2 * PACK], F32, name="vec_" + name)
-            nc.vector.tensor_copy(out=vecs["d"][:], in_=d_raw[:].rearrange("p g t -> p (g t)"))
-            nc.vector.tensor_copy(out=vecs["m"][:], in_=c_raw[:].rearrange("p g t -> p (g t)"))
-            nc.vector.tensor_scalar_max(out=vecs["pos"][:], in0=vecs["m"][:], scalar1=TINY)
-            nc.vector.tensor_scalar_min(out=vecs["neg"][:], in0=vecs["m"][:], scalar1=-TINY)
-            nc.vector.tensor_single_scalar(out=vecs["m"][:], in_=vecs["m"][:], scalar=0.0, op=ALU.is_ge)
-            nc.vector.tensor_tensor(out=vecs["pos"][:], in0=vecs["pos"][:], in1=vecs["neg"][:], op=ALU.subtract)
-            nc.vector.tensor_tensor(out=vecs["pos"][:], in0=vecs["pos"][:], in1=vecs["m"][:], op=ALU.mult)
-            nc.vector.tensor_tensor(out=vecs["c"][:], in0=vecs["pos"][:], in1=vecs["neg"][:], op=ALU.add)
-            nc.vector.reciprocal(out=vecs["ic"][:], in_=vecs["c"][:])
-
-        for half in range(2):
-            for gi in range(2):
-                turn_lam(0, gi, half)
-        group_g(0, 0)
-        group_g(1, 0)
-        g1_codes[0, 0] = quantize(g1[0, 0])
-        scale_lam(0, 0)
-        g1_codes[1, 0] = quantize(g1[1, 0])
-        scale_lam(0, 1)
+        turn_lam(0, 0, 0)
+        turn_lam(0, 1, 0)
+        turn_lam(0, 0, 1)
+        turn_lam(0, 1, 1)
         prepare_vectors()
-        ld_codes[0, 0] = quantize(ld[0, 0])
-        ld_codes[0, 1] = quantize(ld[0, 1])
-        stage1(0, 0)
-        turn_b(0, 0, 0)
-        turn_b(0, 0, 1)
-        step_l2(0, 0)
-        turn_b(0, 1, 0)
-        turn_b(0, 1, 1)
-        group_g(0, 1)
-        step_w(0, 0)
-        step_w2(0, 0)
-        group_g(1, 1)
-        g1_codes[0, 1] = quantize(g1[0, 1])
-        g1_codes[1, 1] = quantize(g1[1, 1])
-        stage1(0, 1)
-        step_l2(0, 1)
+        take_lam(0, 1, 0)
         for half in range(2):
-            for gi in range(2):
-                turn_lam(1, gi, half)
-        step_s2(0, 0)
-        step_w(0, 1)
-        step_w2(0, 1)
-        step_r(0, 0)
-        scale_lam(1, 0)
+            take_lam(0, 0, half)
+        take_lam(0, 1, 1)
+        group_g(0, 0)
+        group_g(1, 0, on_scalar=True)
+        for half in range(2):
+            turn_b(0, 0, half)
+        for half in range(2):
+            turn_b(0, 1, half)
+        quantize_g(0, 0)
+        scale_lam(0, 0)
+        scale_lam(0, 1)
+        load_second_lam()
+        quantize_lam_d(0, 0)
+        quantize_lam_d(0, 1)
+        take_b(0, 0, 0)
+        quantize_g(1, 0)
+        for t in range(4):
+            first_product(0, 0, t)
+        square_lam(0, 1)
+        load_second_b()
+        take_b(0, 0, 1)
+        square_lam(0, 0)
+        for half in range(2):
+            take_b(0, 1, half)
+        group_g(0, 1)
+        group_g(1, 1)
+        for half in range(2):
+            turn_lam(1, 1, half)
+        for half in range(2):
+            turn_lam(1, 0, half)
+        quantize_g(0, 1)
+        for t in range(4):
+            minus_w(0, 0, t)
+        quantize_g(1, 1)
+        take_lam(1, 1, 0)
+        take_lam(1, 0, 0)
+        take_lam(1, 1, 1)
+        take_lam(1, 0, 1)
+        turn_b(1, 1, 0)
+        minus_lam_w(0, 0)
+        turn_g(1, 0, 0)
+        for t in range(4):
+            first_product(0, 1, t)
         scale_lam(1, 1)
-        ld_codes[1, 0] = quantize(ld[1, 0])
-        ld_codes[1, 1] = quantize(ld[1, 1])
-        step_s2(0, 1)
-        step_r(0, 1)
-        stage1(1, 0)
+        scale_lam(1, 0)
+        minus_w(0, 1, 0)
         for half in range(2):
             turn_b(1, 0, half)
-        step_l2(1, 0)
-        step_w(1, 0)
-        step_w2(1, 0)
-        stage1(1, 1)
-        for half in range(2):
-            turn_b(1, 1, half)
-        step_l2(1, 1)
-        step_w(1, 1)
-        step_w2(1, 1)
-        step_x(0, 0)
-        step_s2(1, 0)
-        step_r(1, 0)
-        step_x(0, 1)
-        step_s2(1, 1)
-        step_r(1, 1)
-        step_ri(0, 0)
-        step_ri(0, 1)
-        step_y(0, 0)
-        step_phi(0, 0)
-        step_y(0, 1)
-        step_phi(0, 1)
-        step_x(1, 0)
-        step_x(1, 1)
-        for gj in range(2):
-            for gi in range(2):
-                for half in range(2):
-                    turn_g(gj, gi, half)
-        step_qc(0, 0)
-        step_qc(0, 1)
-        for gj in range(2):
-            for gi in range(2):
-                gT_codes[gj, gi] = quantize(gT[gj, gi])
-        step_hw(0, 0)
-        step_hw(0, 1)
-        step_hl(0, 0)
-        hw_codes[0, 0] = quantize(hw[0, 0])
-        hw_codes[0, 1] = quantize(hw[0, 1])
-        stage2(0, 0)
-        step_hl(0, 1)
-        step_ri(1, 0)
-        step_ri(1, 1)
-        step_y(1, 0)
-        step_phi(1, 0)
-        step_o(0, 0)
-        turn_out(0, 0)
-        step_ob(0, 0, False)
-        stage2(0, 1)
-        step_y(1, 1)
-        step_phi(1, 1)
-        step_o(0, 1)
-        turn_out(0, 1)
-        step_ob(0, 1, False)
-        step_qc(1, 0)
-        step_qc(1, 1)
-        step_oq(0, 0)
-        step_hw(1, 0)
-        step_hw(1, 1)
-        hw_codes[1, 0] = quantize(hw[1, 0])
-        step_oq(0, 1)
-        hw_codes[1, 1] = quantize(hw[1, 1])
-        stage2(1, 0)
-        step_hl(1, 0)
-        step_hl(1, 1)
-        step_o(1, 0)
-        turn_out(1, 0)
-        stage2(1, 1)
-        step_o(1, 1)
-        turn_out(1, 1)
-        step_ob(1, 0, True)
-        step_oq(1, 0)
-        step_ob(1, 1, True)
-        step_oq(1, 1)
+        quantize_lam_d(1, 0)
+        square_w(0, 0)
+        square_lam(1, 0)
+        for t in range(1, 3):
+            minus_w(0, 1, t)
+        take_b(1, 1, 0)
+        take_g(1, 0, 0)
+        turn_b(1, 1, 1)
+        quantize_lam_d(1, 1)
+        minus_w(0, 1, 3)
+        sum_squares(0, 0)
+        first_product(1, 0, 0)
+        first_product(1, 1, 0)
+        square_w(0, 1)
+        take_b(1, 0, 0)
+        take_b(1, 1, 1)
+        take_b(1, 0, 1)
+        turn_g(0, 0, 0)
+        minus_lam_w(0, 1)
+        minus_w(1, 1, 0)
+        sum_squares(0, 1)
+        root(0, 0)
+        root(0, 1)
+        minus_w(1, 0, 0)
+        first_product(1, 1, 1)
+        first_product(1, 0, 1)
+        minus_w(1, 0, 1)
+        minus_w(1, 1, 1)
+        turn_g(1, 0, 1)
+        r_minus_w_0(0, 0)
+        take_g(0, 0, 0)
+        take_g(1, 0, 1)
+        first_product(1, 1, 2)
+        for t in range(2, 4):
+            first_product(1, 0, t)
+        first_product(1, 1, 3)
+        for t in range(2, 4):
+            minus_w(1, 0, t)
+        minus_w(1, 1, 2)
+        turn_g(0, 1, 0)
+        turn_g(0, 0, 1)
+        turn_g(0, 1, 1)
+        turn_g(1, 1, 0)
+        r_minus_w_0(0, 1)
+        inverse_root(0, 0)
+        minus_w(1, 1, 3)
+        take_g(0, 0, 1)
+        inverse_root(0, 1)
+        quantize_g_t(1, 0)
+        ratio(0, 0)
+        ratio(0, 1)
+        square_w(1, 0)
+        qc_0(0, 0)
+        take_g(0, 1, 0)
+        sum_squares(1, 0)
+        multiply_hw_c(0, 0)
+        qc_0(0, 1)
+        square_lam(1, 1)
+        quantize_g_t(0, 0)
+        quantize_hw(0, 0)
+        multiply_hw_c(0, 1)
+        take_g(0, 1, 1)
+        for t in range(2):
+            second_product(0, 0, t, 0)
+        square_w(1, 1)
+        lam_q(0, 1)
+        quantize_hw(0, 1)
+        second_product(0, 0, 0, 1)
+        second_product(0, 0, 2, 0)
+        for t in range(1, 3):
+            second_product(0, 0, t, 1)
+        second_product(0, 0, 3, 0)
+        second_product(0, 0, 3, 1)
+        root(1, 0)
+        take_g(1, 1, 0)
+        lam_q(0, 0)
+        quantize_g_t(0, 1)
+        sum_squares(1, 1)
+        for t in range(2):
+            scale_back(0, 0, t)
+        turn_g(1, 1, 1)
+        take_g(1, 1, 1)
+        for t in range(2, 4):
+            scale_back(0, 0, t)
+        second_product(0, 1, 0, 0)
+        root(1, 1)
+        r_minus_lam(1, 0)
+        inverse_root(1, 0)
+        quantize_g_t(1, 1)
+        r_minus_w_1(1, 0)
+        r_minus_lam(1, 1)
+        add_turned(0, 0, 0)
+        for t in range(1, 3):
+            second_product(0, 1, t, 0)
+        second_product(0, 1, 0, 1)
+        second_product(0, 1, 3, 0)
+        for t in range(1, 4):
+            second_product(0, 1, t, 1)
+        minus_phi(1, 0)
+        copy_out(0, 0, 0)
+        for t in range(4):
+            scale_back(0, 1, t)
+        for slot in range(1, 4):
+            add_turned(0, 0, slot)
+        add_turned(0, 1, 0)
+        r_minus_w_1(1, 1)
+        qc_1(1, 0)
+        for slot in range(1, 4):
+            copy_out(0, 0, slot)
+        copy_out(0, 1, 0)
+        for slot in range(1, 4):
+            add_turned(0, 1, slot)
+        minus_phi(1, 1)
+        inverse_root(1, 1)
+        multiply_hw_c(1, 0)
+        qc_1(1, 1)
+        quantize_hw(1, 0)
+        pack_out(0, 0, on_vector=False)
+        multiply_hw_c(1, 1)
+        store_out(0, 0)
+        quantize_hw(1, 1)
+        for slot in range(1, 4):
+            copy_out(0, 1, slot)
+        second_product(1, 0, 0, 0)
+        second_product(1, 1, 0, 0)
+        for t in range(1, 3):
+            second_product(1, 0, t, 0)
+        for t in range(2):
+            second_product(1, 0, t, 1)
+        second_product(1, 1, 0, 1)
+        second_product(1, 0, 2, 1)
+        pack_out(0, 1, on_vector=False)
+        invert_c()
+        scale_back(1, 0, 0)
+        scale_back(1, 1, 0)
+        scale_back(1, 0, 2)
+        store_out(0, 1)
+        second_product(1, 1, 1, 0)
+        second_product(1, 1, 1, 1)
+        second_product(1, 0, 3, 0)
+        second_product(1, 0, 3, 1)
+        quantize_out(0, 0)
+        minus_hl(1, 0)
+        scale_back(1, 0, 1, on_vector=True)
+        scale_back(1, 0, 3)
+        scale_back(1, 1, 1)
+        quantize_out(0, 1)
+        second_product(1, 1, 2, 0)
+        for slot in range(2):
+            add_turned(1, 0, slot)
+        for slot in range(2):
+            copy_out(1, 0, slot)
+        second_product(1, 1, 3, 0)
+        for t in range(2, 4):
+            second_product(1, 1, t, 1)
+        minus_hl(1, 1)
+        for t in range(2, 4):
+            scale_back(1, 1, t)
+        for slot in range(2, 4):
+            add_turned(1, 0, slot)
+        for slot in range(2):
+            add_turned(1, 1, slot)
+        for slot in range(2, 4):
+            copy_out(1, 0, slot)
+        for slot in range(2):
+            copy_out(1, 1, slot)
+        store_out(1, 0)
+        pack_out(1, 0, on_vector=True)
+        for slot in range(2, 4):
+            add_turned(1, 1, slot)
+        copy_out(1, 1, 2)
+        quantize_out(1, 0)
+        copy_out(1, 1, 3, on_vector=True)
+        store_out(1, 1)
+        pack_out(1, 1, on_vector=True)
+        quantize_out(1, 1)

from contextlib import ExitStack

import concourse.mybir as mybir
from concourse.masks import make_identity

S = 1024
N = 1024
P = 128
PACK = 4
GROUP = P * PACK
SMOOTH = 0.02
TINY = 1e-30

FLOPS = 2 * 2 * S * N * N

F32 = mybir.dt.float32
BF16 = mybir.dt.bfloat16
U32 = mybir.dt.uint32
I32 = mybir.dt.int32
U8 = mybir.dt.uint8
FP8X4 = mybir.dt.float8_e4m3fn_x4
ALU = mybir.AluOpType
FUNC = mybir.ActivationFunctionType


def tile_fischerburmeisterlcpmeritgradientequilib_x1_kernel(tc, lam, g, d, c, b, out_0, out_1, out_2):
    nc = tc.nc
    with ExitStack() as ctx:
        const = ctx.enter_context(tc.tile_pool(name="const", bufs=1))
        natural = ctx.enter_context(tc.tile_pool(name="natural", bufs=1))
        packed = ctx.enter_context(tc.tile_pool(name="packed", bufs=4))
        quantized = ctx.enter_context(tc.tile_pool(name="quantized", bufs=4))
        turned = ctx.enter_context(tc.tile_pool(name="turned", bufs=4))
        psum = ctx.enter_context(tc.psum_pool(name="psum", bufs=4))

        identity = const.tile([P, P], F32, name="identity")
        make_identity(nc, identity[:])

        ctx.enter_context(tc.manual_schedule())

        lam_rows, b_rows, g_rows = {}, {}, {}

        def load_g(gi, gj):
            g_rows[gi, gj] = natural.tile([P, PACK, GROUP], BF16, name="g_rows", tag="quarter", bufs=4)
            nc.sync.dma_start(
                out=g_rows[gi, gj][:],
                in_=g[gi * GROUP : (gi + 1) * GROUP, gj * GROUP : (gj + 1) * GROUP].rearrange("(p t) j -> p t j", t=PACK),
            )

        def load_rows(x, gs, k, tile, slots=slice(0, PACK)):
            rows = x[gs * GROUP : (gs + 1) * GROUP, k * GROUP : (k + 1) * GROUP].rearrange("(p t) i -> p t i", t=PACK)
            nc.sync.dma_start(out=tile[:, k, slots, :], in_=rows[:, slots, :])

        def new_lam_rows(gs):
            lam_rows[gs] = natural.tile([P, 2, PACK, GROUP], BF16, name="lam_rows", tag="lam_then_out")

        def new_b_rows(gs):
            b_rows[gs] = natural.tile([P, 2, PACK, GROUP], BF16, name="b_rows", tag="b_then_out")

        def load_second_lam():
            new_lam_rows(1)
            for k in range(2):
                load_rows(lam, 1, k, lam_rows[1])

        def load_second_b():
            new_b_rows(1)
            for k in range(2):
                load_rows(b, 1, k, b_rows[1])

        new_lam_rows(0)
        new_b_rows(0)
        c_bf16 = const.tile([P, 2, PACK], BF16, name="c_bf16")
        d_bf16 = const.tile([P, 2, PACK], BF16, name="d_bf16")
        for k in range(2):
            load_rows(lam, 0, k, lam_rows[0], slice(0, 2))
        load_g(0, 0)
        for k in range(2):
            load_rows(lam, 0, k, lam_rows[0], slice(2, 4))
        nc.sync.dma_start(out=d_bf16[:], in_=d.rearrange("(g p t) -> p g t", p=P, t=PACK))
        load_g(1, 0)
        nc.sync.dma_start(out=c_bf16[:], in_=c.rearrange("(g p t) -> p g t", p=P, t=PACK))
        for k in range(2):
            load_rows(b, 0, k, b_rows[0])
        load_g(0, 1)
        load_g(1, 1)

        vectors = {}

        def column(name, group, t):
            return vectors[name][:, PACK * group + t : PACK * group + t + 1]

        def prepare_vectors():
            for name in ("c", "minus_d", "minus_c", "upper", "lower", "minus_1_over_c"):
                vectors[name] = const.tile([P, 2 * PACK], F32, name="vector_" + name)
            c_flat = c_bf16[:].rearrange("p g t -> p (g t)")
            d_flat = d_bf16[:].rearrange("p g t -> p (g t)")
            nc.gpsimd.tensor_scalar(out=vectors["minus_d"][:], in0=d_flat, scalar1=-1.0, scalar2=0.0, op0=ALU.mult, op1=ALU.add)
            nc.gpsimd.tensor_scalar(out=vectors["c"][:], in0=c_flat, scalar1=0.0, scalar2=1.0, op0=ALU.is_ge, op1=ALU.mult)
            nc.gpsimd.tensor_scalar(out=vectors["upper"][:], in0=c_flat, scalar1=TINY, scalar2=1.0, op0=ALU.max, op1=ALU.mult)
            nc.gpsimd.tensor_scalar(out=vectors["lower"][:], in0=c_flat, scalar1=-TINY, scalar2=1.0, op0=ALU.min, op1=ALU.mult)
            nc.gpsimd.tensor_tensor(out=vectors["upper"][:], in0=vectors["upper"][:], in1=vectors["lower"][:], op=ALU.subtract)
            nc.gpsimd.tensor_tensor(out=vectors["upper"][:], in0=vectors["upper"][:], in1=vectors["c"][:], op=ALU.mult)
            nc.gpsimd.tensor_tensor(out=vectors["c"][:], in0=vectors["upper"][:], in1=vectors["lower"][:], op=ALU.add)
            nc.gpsimd.tensor_scalar(out=vectors["minus_c"][:], in0=vectors["c"][:], scalar1=-1.0, scalar2=0.0, op0=ALU.mult, op1=ALU.add)

        def invert_c():
            nc.vector.reciprocal(out=vectors["minus_1_over_c"][:], in_=vectors["minus_c"][:])

        banks = {}
        lam_t, b_t, g_t = {}, {}, {}

        def turn(key, rows):
            half = key[-1]
            banks[key] = psum.tile([P, 2, 2 * P], F32, name="turn_bank", tag="turn")
            words = rows.bitcast(F32)
            for n in range(2):
                for u in range(2):
                    nc.tensor.transpose(banks[key][:, u, n * P : (n + 1) * P], words[:, 2 * half + n, u::2], identity[:])

        def turn_lam(gs, gi, half):
            turn(("lam", gs, gi, half), lam_rows[gs][:, gi])

        def turn_b(gs, gj, half):
            turn(("b", gs, gj, half), b_rows[gs][:, gj])

        def turn_g(gj, gi, half):
            turn(("g", gj, gi, half), g_rows[gi, gj][:])

        def copy_words(out, in_, on_vector):
            (nc.vector.tensor_copy if on_vector else nc.scalar.copy)(out=out, in_=in_)

        def take_words(store, key, bufs, pool, on_vector):
            name, x, y, half = key
            if (x, y) not in store:
                store[x, y] = pool.tile([P, GROUP * PACK], BF16, name=name + "_t", tag=name + "_t", align_bytes=64, bufs=bufs)
            words = store[x, y][:].rearrange("p (u s e) -> p u (s e)", u=2, e=2).bitcast(F32)
            copy_words(words[:, :, half * 2 * P : (half + 1) * 2 * P], banks[key][:], on_vector)

        def take_lam(gs, gi, half, on_vector=False):
            take_words(lam_t, ("lam", gs, gi, half), 4, turned, on_vector)

        def take_b(gs, gj, half, on_vector=False):
            take_words(b_t, ("b", gs, gj, half), 2, packed, on_vector)

        def new_packed(name):
            return packed.tile([P, GROUP * PACK], BF16, name=name, tag="packed", align_bytes=64)

        def take_g(gj, gi, half, on_vector=False):
            if (gj, gi) not in g_t:
                g_t[gj, gi] = new_packed("g_t")
            words = g_t[gj, gi][:].rearrange("p (i t) -> p i t", t=PACK).bitcast(F32)
            copy_words(words[:, half * 2 * P : (half + 1) * 2 * P, :], banks["g", gj, gi, half][:].rearrange("p u r -> p r u"), on_vector)

        def by_t(tile):
            return tile[:].rearrange("p (u s e) -> p u e s", u=2, e=2)

        def split_t(tile):
            return tile[:].rearrange("p (u e) s -> p u e s", e=2)

        g_codes, g_t_codes, lam_d_codes, hw_codes = {}, {}, {}, {}
        g_packed, lam_d = {}, {}

        def quantize(values, kind):
            words = quantized.tile([P, GROUP], U32, name="words", tag="words_" + kind, align_bytes=64)
            scales = quantized.tile([P, GROUP], U8, name="scales", tag="scales_" + kind, align_bytes=64)
            nc.vector.quantize_mx(out=words[:].bitcast(FP8X4), scales=scales[:], in_=values[:])
            return words, scales

        def group_g(gi, gj, on_scalar=False):
            g_packed[gi, gj] = new_packed("g_packed")
            (nc.scalar.copy if on_scalar else nc.vector.tensor_copy)(
                out=g_packed[gi, gj][:].rearrange("p (t m i) -> p t m i", t=PACK, i=PACK),
                in_=g_rows[gi, gj][:].rearrange("p i (m t) -> p t m i", t=PACK),
            )

        def quantize_g(gi, gj):
            g_codes[gi, gj] = quantize(g_packed[gi, gj], "g")

        def quantize_g_t(gj, gi):
            g_t_codes[gj, gi] = quantize(g_t[gj, gi], "g")

        def scale_lam(gs, gi):
            lam_d[gs, gi] = new_packed("lam_d")
            nc.vector.tensor_tensor(
                out=lam_d[gs, gi][:].rearrange("p (s u e) -> p s u e", u=2, e=2),
                in0=lam_t[gs, gi][:].rearrange("p (u s e) -> p s u e", u=2, e=2),
                in1=d_bf16[:, gi, :].rearrange("p (u e) -> p u e", e=2).unsqueeze(1).to_broadcast([P, GROUP, 2, 2]),
                op=ALU.mult,
            )

        def quantize_lam_d(gs, gi):
            lam_d_codes[gs, gi] = quantize(lam_d[gs, gi], "samples")

        products = {}

        def pass_mx(bank, left, t, right, first, last):
            cols = slice(t * P, (t + 1) * P)
            nc.tensor.matmul_mx(
                out=bank[:],
                lhsT=left[0][:, cols].bitcast(FP8X4),
                lhsT_scale=left[1][:, cols],
                rhs=right[0][:].bitcast(FP8X4),
                rhs_scale=right[1][:],
                start=first,
                stop=last,
            )

        def first_product(gs, gj, t):
            products[gs, gj, t] = psum.tile([P, GROUP], F32, name="product", tag="product")
            for gi in range(2):
                pass_mx(products[gs, gj, t], g_codes[gi, gj], t, lam_d_codes[gs, gi], gi == 0, gi == 1)

        w_tile, sum_tile, root_tile, term_tile, w_squared, qc_tile = {}, {}, {}, {}, {}, {}

        def new_turned(name, tag, bufs=4):
            return turned.tile([P, PACK, GROUP], F32, name=name, tag=tag, bufs=bufs)

        def minus_w(gs, gj, t):
            if (gs, gj) not in w_tile:
                w_tile[gs, gj] = new_turned("w_tile", "w")
            nc.vector.scalar_tensor_tensor(
                out=w_tile[gs, gj][:, t, :],
                in0=products[gs, gj, t][:],
                scalar=column("minus_c", gj, t),
                in1=by_t(b_t[gs, gj])[:, t // 2, t % 2, :],
                op0=ALU.mult,
                op1=ALU.subtract,
            )

        def square_lam(gs, gj):
            sum_tile[gs, gj] = new_turned("sum_tile", "sum")
            nc.scalar.activation(out=split_t(sum_tile[gs, gj]), in_=by_t(lam_t[gs, gj]), func=FUNC.Square)

        def square_w(gs, gj):
            w_squared[gs, gj] = new_turned("w_squared", "short", 2)
            nc.scalar.activation(out=w_squared[gs, gj][:], in_=w_tile[gs, gj][:], func=FUNC.Square)

        def sum_squares(gs, gj):
            nc.vector.scalar_tensor_tensor(
                out=sum_tile[gs, gj][:], in0=w_squared[gs, gj][:], scalar=SMOOTH, in1=sum_tile[gs, gj][:], op0=ALU.add, op1=ALU.add
            )

        def root(gs, gj):
            root_tile[gs, gj] = new_turned("root_tile", "root")
            nc.scalar.activation(out=root_tile[gs, gj][:], in_=sum_tile[gs, gj][:], func=FUNC.Sqrt)

        def inverse_root(gs, gj):
            nc.scalar.activation(out=sum_tile[gs, gj][:], in_=sum_tile[gs, gj][:], func=FUNC.Abs_reciprocal_sqrt)

        def minus_lam_w(gs, gj):
            term_tile[gs, gj] = new_turned("term_tile", "term")
            nc.vector.tensor_tensor(out=split_t(term_tile[gs, gj]), in0=split_t(w_tile[gs, gj]), in1=by_t(lam_t[gs, gj]), op=ALU.subtract)

        def r_minus_w_0(gs, gj):
            nc.vector.tensor_tensor(out=w_tile[gs, gj][:], in0=root_tile[gs, gj][:], in1=w_tile[gs, gj][:], op=ALU.add)

        def ratio(gs, gj):
            nc.vector.scalar_tensor_tensor(
                out=sum_tile[gs, gj][:], in0=term_tile[gs, gj][:], scalar=-1.0, in1=sum_tile[gs, gj][:], op0=ALU.mult, op1=ALU.mult
            )

        def qc_0(gs, gj):
            qc_tile[gs, gj] = new_turned("qc_tile", "short", 2)
            for t in range(PACK):
                nc.scalar.activation(
                    out=qc_tile[gs, gj][:, t, :],
                    in_=sum_tile[gs, gj][:, t, :],
                    func=FUNC.Identity,
                    scale=column("c", gj, t),
                    bias=column("minus_c", gj, t),
                )

        def lam_q(gs, gj):
            for u in range(2):
                part = split_t(sum_tile[gs, gj])[:, u]
                nc.vector.scalar_tensor_tensor(
                    out=part, in0=part, scalar=1.0, in1=by_t(lam_t[gs, gj])[:, u], op0=ALU.subtract, op1=ALU.mult
                )

        def r_minus_lam(gs, gj):
            term_tile[gs, gj] = new_turned("term_tile", "term")
            nc.vector.tensor_tensor(out=split_t(term_tile[gs, gj]), in0=split_t(root_tile[gs, gj]), in1=by_t(lam_t[gs, gj]), op=ALU.subtract)

        def r_minus_w_1(gs, gj):
            nc.vector.tensor_tensor(out=root_tile[gs, gj][:], in0=root_tile[gs, gj][:], in1=w_tile[gs, gj][:], op=ALU.add)

        def minus_phi(gs, gj):
            nc.vector.tensor_tensor(out=w_tile[gs, gj][:], in0=w_tile[gs, gj][:], in1=term_tile[gs, gj][:], op=ALU.add)

        def qc_1(gs, gj):
            for t in range(PACK):
                nc.vector.scalar_tensor_tensor(
                    out=w_tile[gs, gj][:, t, :],
                    in0=w_tile[gs, gj][:, t, :],
                    scalar=column("minus_c", gj, t),
                    in1=sum_tile[gs, gj][:, t, :],
                    op0=ALU.mult,
                    op1=ALU.mult,
                )

        def minus_hl(gs, gj):
            for t in range(PACK):
                nc.vector.scalar_tensor_tensor(
                    out=term_tile[gs, gj][:, t, :],
                    in0=w_tile[gs, gj][:, t, :],
                    scalar=column("minus_1_over_c", gj, t),
                    in1=term_tile[gs, gj][:, t, :],
                    op0=ALU.mult,
                    op1=ALU.mult,
                )

        hw_c = {}

        def interleave(tile):
            return tile[:].rearrange("p t (n k) -> p n t k", k=4)

        def interleaved(tile):
            return tile[:].rearrange("p (n k t) -> p n t k", k=4, t=PACK)

        def multiply_hw_c(gs, gj):
            hw_c[gs, gj] = new_packed("hw_c")
            qc, r_minus_w = (qc_tile, w_tile) if gs == 0 else (w_tile, root_tile)
            nc.vector.tensor_tensor(
                out=interleaved(hw_c[gs, gj]), in0=interleave(qc[gs, gj]), in1=interleave(r_minus_w[gs, gj]), op=ALU.mult
            )

        def quantize_hw(gs, gj):
            hw_codes[gs, gj] = quantize(hw_c[gs, gj], "samples")

        back = {}

        def second_product(gs, gi, t, gj):
            if gj == 0:
                back[gs, gi, t] = psum.tile([P, GROUP], F32, name="product", tag="product")
            pass_mx(back[gs, gi, t], g_t_codes[gj, gi], t, hw_codes[gs, gj], gj == 0, gj == 1)

        minus_d_back = {}

        def scale_back(gs, gi, t, on_vector=False):
            if (gs, gi, t // 2) not in minus_d_back:
                minus_d_back[gs, gi, t // 2] = natural.tile([P, 2, GROUP], F32, name="minus_d_back", tag="quarter", bufs=4)
            target = minus_d_back[gs, gi, t // 2][:, t % 2, :]
            if on_vector:
                nc.vector.tensor_scalar_mul(out=target, in0=back[gs, gi, t][:], scalar1=column("minus_d", gi, t))
            else:
                nc.scalar.activation(out=target, in_=back[gs, gi, t][:], func=FUNC.Copy, scale=column("minus_d", gi, t))

        out_banks, out_rows, out_packed = {}, {}, {}

        def add_turned(gs, gi, slot):
            bank = psum.tile([P, PACK, P], F32, name="out_bank", tag="turn")
            for t in range(PACK):
                addends = [term_tile[gs, gi][:, t, :], minus_d_back[gs, gi, t // 2][:, t % 2, :]]
                if gs == 0:
                    addends += [root_tile[gs, gi][:, t, :], sum_tile[gs, gi][:, t, :]]
                for n, addend in enumerate(addends):
                    nc.tensor.matmul(
                        bank[:, t, :],
                        lhsT=addend[:, slot * P : (slot + 1) * P],
                        rhs=identity[:],
                        is_transpose=True,
                        start=n == 0,
                        stop=n == len(addends) - 1,
                    )
            out_banks[gs, gi, slot] = bank

        def copy_out(gs, gi, slot, on_vector=False):
            if (gs, gi) not in out_rows:
                out_rows[gs, gi] = natural.tile([P, PACK, GROUP], F32, name="out_rows", tag=("lam_then_out", "b_then_out")[gi])
            target = out_rows[gs, gi][:, slot, :].rearrange("p (m t) -> p m t", t=PACK)
            source = out_banks[gs, gi, slot][:].rearrange("p t m -> p m t")
            if on_vector:
                nc.vector.tensor_scalar_mul(out=target, in0=source, scalar1=-1.0)
            else:
                nc.scalar.activation(out=target, in_=source, func=FUNC.Copy, scale=-1.0)

        def store_out(gs, gi):
            nc.sync.dma_start(
                out=out_0[gs * GROUP : (gs + 1) * GROUP, gi * GROUP : (gi + 1) * GROUP].rearrange("(p t) i -> p t i", t=PACK),
                in_=out_rows[gs, gi][:],
            )

        def pack_out(gs, gi, on_vector):
            out_packed[gs, gi] = new_packed("out_packed")
            copy = nc.vector.tensor_copy if on_vector else nc.scalar.copy
            copy(out=interleaved(out_packed[gs, gi]), in_=interleave(out_rows[gs, gi]))

        def quantize_out(gs, gi):
            words, scales = quantize(out_packed[gs, gi], "samples")
            cols = slice(gi * GROUP, (gi + 1) * GROUP)
            nc.sync.dma_start(out=out_1[gs, :, cols, :].rearrange("p m t -> p (m t)").bitcast(I32), in_=words[:].bitcast(I32))
            for quadrant in range(4):
                nc.sync.dma_start(
                    out=out_2[gs, 4 * quadrant : 4 * quadrant + 4, cols].bitcast(I32),
                    in_=scales[32 * quadrant : 32 * quadrant + 4, :].bitcast(I32),
                )

        turn_lam(0, 0, 0)
        turn_lam(0, 1, 0)
        turn_lam(0, 0, 1)
        turn_lam(0, 1, 1)
        prepare_vectors()
        take_lam(0, 1, 0)
        for half in range(2):
            take_lam(0, 0, half)
        take_lam(0, 1, 1)
        group_g(0, 0)
        group_g(1, 0, on_scalar=True)
        for half in range(2):
            turn_b(0, 0, half)
        for half in range(2):
            turn_b(0, 1, half)
        quantize_g(0, 0)
        scale_lam(0, 0)
        scale_lam(0, 1)
        load_second_lam()
        quantize_lam_d(0, 0)
        quantize_lam_d(0, 1)
        take_b(0, 0, 0)
        quantize_g(1, 0)
        for t in range(4):
            first_product(0, 0, t)
        square_lam(0, 1)
        load_second_b()
        take_b(0, 0, 1)
        square_lam(0, 0)
        for half in range(2):
            take_b(0, 1, half)
        group_g(0, 1)
        group_g(1, 1)
        for half in range(2):
            turn_lam(1, 1, half)
        for half in range(2):
            turn_lam(1, 0, half)
        quantize_g(0, 1)
        for t in range(4):
            minus_w(0, 0, t)
        quantize_g(1, 1)
        take_lam(1, 1, 0)
        take_lam(1, 0, 0)
        take_lam(1, 1, 1)
        take_lam(1, 0, 1)
        turn_b(1, 1, 0)
        minus_lam_w(0, 0)
        turn_g(1, 0, 0)
        for t in range(4):
            first_product(0, 1, t)
        scale_lam(1, 1)
        scale_lam(1, 0)
        minus_w(0, 1, 0)
        for half in range(2):
            turn_b(1, 0, half)
        quantize_lam_d(1, 0)
        square_w(0, 0)
        square_lam(1, 0)
        for t in range(1, 3):
            minus_w(0, 1, t)
        take_b(1, 1, 0)
        take_g(1, 0, 0)
        turn_b(1, 1, 1)
        quantize_lam_d(1, 1)
        minus_w(0, 1, 3)
        sum_squares(0, 0)
        first_product(1, 0, 0)
        first_product(1, 1, 0)
        square_w(0, 1)
        take_b(1, 0, 0)
        take_b(1, 1, 1)
        take_b(1, 0, 1)
        turn_g(0, 0, 0)
        minus_lam_w(0, 1)
        minus_w(1, 1, 0)
        sum_squares(0, 1)
        root(0, 0)
        root(0, 1)
        minus_w(1, 0, 0)
        first_product(1, 1, 1)
        first_product(1, 0, 1)
        minus_w(1, 0, 1)
        minus_w(1, 1, 1)
        turn_g(1, 0, 1)
        r_minus_w_0(0, 0)
        take_g(0, 0, 0)
        take_g(1, 0, 1)
        first_product(1, 1, 2)
        for t in range(2, 4):
            first_product(1, 0, t)
        first_product(1, 1, 3)
        for t in range(2, 4):
            minus_w(1, 0, t)
        minus_w(1, 1, 2)
        turn_g(0, 1, 0)
        turn_g(0, 0, 1)
        turn_g(0, 1, 1)
        turn_g(1, 1, 0)
        r_minus_w_0(0, 1)
        inverse_root(0, 0)
        minus_w(1, 1, 3)
        take_g(0, 0, 1)
        inverse_root(0, 1)
        quantize_g_t(1, 0)
        ratio(0, 0)
        ratio(0, 1)
        square_w(1, 0)
        qc_0(0, 0)
        take_g(0, 1, 0)
        sum_squares(1, 0)
        multiply_hw_c(0, 0)
        qc_0(0, 1)
        square_lam(1, 1)
        quantize_g_t(0, 0)
        quantize_hw(0, 0)
        multiply_hw_c(0, 1)
        take_g(0, 1, 1)
        for t in range(2):
            second_product(0, 0, t, 0)
        square_w(1, 1)
        lam_q(0, 1)
        quantize_hw(0, 1)
        second_product(0, 0, 0, 1)
        second_product(0, 0, 2, 0)
        for t in range(1, 3):
            second_product(0, 0, t, 1)
        second_product(0, 0, 3, 0)
        second_product(0, 0, 3, 1)
        root(1, 0)
        take_g(1, 1, 0)
        lam_q(0, 0)
        quantize_g_t(0, 1)
        sum_squares(1, 1)
        for t in range(2):
            scale_back(0, 0, t)
        turn_g(1, 1, 1)
        take_g(1, 1, 1)
        for t in range(2, 4):
            scale_back(0, 0, t)
        second_product(0, 1, 0, 0)
        root(1, 1)
        r_minus_lam(1, 0)
        inverse_root(1, 0)
        quantize_g_t(1, 1)
        r_minus_w_1(1, 0)
        r_minus_lam(1, 1)
        add_turned(0, 0, 0)
        for t in range(1, 3):
            second_product(0, 1, t, 0)
        second_product(0, 1, 0, 1)
        second_product(0, 1, 3, 0)
        for t in range(1, 4):
            second_product(0, 1, t, 1)
        minus_phi(1, 0)
        copy_out(0, 0, 0)
        for t in range(4):
            scale_back(0, 1, t)
        for slot in range(1, 4):
            add_turned(0, 0, slot)
        add_turned(0, 1, 0)
        r_minus_w_1(1, 1)
        qc_1(1, 0)
        for slot in range(1, 4):
            copy_out(0, 0, slot)
        copy_out(0, 1, 0)
        for slot in range(1, 4):
            add_turned(0, 1, slot)
        minus_phi(1, 1)
        inverse_root(1, 1)
        multiply_hw_c(1, 0)
        qc_1(1, 1)
        quantize_hw(1, 0)
        pack_out(0, 0, on_vector=False)
        multiply_hw_c(1, 1)
        store_out(0, 0)
        quantize_hw(1, 1)
        for slot in range(1, 4):
            copy_out(0, 1, slot)
        second_product(1, 0, 0, 0)
        second_product(1, 1, 0, 0)
        for t in range(1, 3):
            second_product(1, 0, t, 0)
        for t in range(2):
            second_product(1, 0, t, 1)
        second_product(1, 1, 0, 1)
        second_product(1, 0, 2, 1)
        pack_out(0, 1, on_vector=False)
        invert_c()
        scale_back(1, 0, 0)
        scale_back(1, 1, 0)
        scale_back(1, 0, 2)
        store_out(0, 1)
        second_product(1, 1, 1, 0)
        second_product(1, 1, 1, 1)
        second_product(1, 0, 3, 0)
        second_product(1, 0, 3, 1)
        quantize_out(0, 0)
        minus_hl(1, 0)
        scale_back(1, 0, 1, on_vector=True)
        scale_back(1, 0, 3)
        scale_back(1, 1, 1)
        quantize_out(0, 1)
        second_product(1, 1, 2, 0)
        for slot in range(2):
            add_turned(1, 0, slot)
        for slot in range(2):
            copy_out(1, 0, slot)
        second_product(1, 1, 3, 0)
        for t in range(2, 4):
            second_product(1, 1, t, 1)
        minus_hl(1, 1)
        for t in range(2, 4):
            scale_back(1, 1, t)
        for slot in range(2, 4):
            add_turned(1, 0, slot)
        for slot in range(2):
            add_turned(1, 1, slot)
        for slot in range(2, 4):
            copy_out(1, 0, slot)
        for slot in range(2):
            copy_out(1, 1, slot)
        store_out(1, 0)
        pack_out(1, 0, on_vector=True)
        for slot in range(2, 4):
            add_turned(1, 1, slot)
        copy_out(1, 1, 2)
        quantize_out(1, 0)
        copy_out(1, 1, 3, on_vector=True)
        store_out(1, 1)
        pack_out(1, 1, on_vector=True)
        quantize_out(1, 1)
